import numpy as np
import ml_dtypes

BF16 = ml_dtypes.bfloat16


def bf(x):
    return np.asarray(x, np.float32).astype(BF16)


def f32(x):
    return np.asarray(x, np.float32)


def f64(x):
    return np.asarray(x).astype(np.float64)


def striped(idx):
    return np.tile(idx.reshape(-1, 16).T, (8, 1))


S, K, M, N = 256, 128, 512, 128


def setup_inputs():
    return {"base": bf(np.random.standard_normal((M, S))), "x": bf(np.random.standard_normal((K, N))), "w": bf(np.random.standard_normal((K, M)) / np.sqrt(K)), "offs": striped(np.random.permutation(S)[:N])}


def reference(base, x, w, offs):
    idx = offs[:16].T.reshape(-1)
    z = f64(base).copy()
    z[:, idx] += f64(w).T @ f64(x)
    return z

@@ -1,0 +1,50 @@
+import concourse.mybir as mybir
+from concourse.masks import make_identity
+
+BF16, F32, U16 = mybir.dt.bfloat16, mybir.dt.float32, mybir.dt.uint16
+
+P = 128
+TOKENS = 256
+FEATURES = 512
+LISTED = 128
+BLOCKS = FEATURES // P
+
+FLOPS = 2 * P * FEATURES * LISTED
+
+
+def tile_scatter_matmul_kernel(tc, base, x, w, offs, out):
+    nc = tc.nc
+    base_blocks = base.rearrange("(a p) s -> p a s", p=P)
+    with (
+        tc.tile_pool(name="held", bufs=1) as held,
+        tc.psum_pool(name="banks", bufs=1) as banks,
+    ):
+        offsets = held.tile([P, LISTED // 16], U16, name="offsets")
+        nc.sync.dma_start(offsets[:], offs)
+        x_tile = held.tile([P, LISTED], BF16, name="x_tile")
+        nc.sync.dma_start(x_tile[:], x)
+        base_tile = held.tile([P, BLOCKS, TOKENS], BF16, name="base_tile")
+        nc.scalar.dma_start(base_tile[:], base_blocks)
+        identity = held.tile([P, P], BF16, name="identity")
+        make_identity(nc, identity[:])
+        w_tile = held.tile([P, FEATURES], BF16, name="w_tile")
+        nc.gpsimd.dma_start(w_tile[:], w)
+
+        windows = [banks.tile([P, TOKENS], F32, name=f"window{a}") for a in range(BLOCKS)]
+
+        for a in range(BLOCKS):
+            nc.tensor.matmul(windows[a][:], identity[:], base_tile[:, a, :], start=True, stop=False)
+
+        for a in range(BLOCKS):
+            nc.tensor.matmul(
+                windows[a][:].indirect(offsets[:]),
+                w_tile[:, a * P : (a + 1) * P],
+                x_tile[:],
+                start=False,
+                stop=True,
+            )
+
+        for a in range(BLOCKS):
+            z_tile = held.tile([P, TOKENS], F32, name=f"z_tile{a}")
+            nc.vector.tensor_copy(z_tile[:], windows[a][:])
+            nc.sync.dma_start(out[a * P : (a + 1) * P, :], z_tile[:])

@@ -14,26 +14,27 @@ FLOPS = 2 * P * FEATURES * LISTED
 
 def tile_scatter_matmul_kernel(tc, base, x, w, offs, out):
     nc = tc.nc
-    base_blocks = base.rearrange("(a p) s -> p a s", p=P)
     with (
         tc.tile_pool(name="held", bufs=1) as held,
         tc.psum_pool(name="banks", bufs=1) as banks,
     ):
+        base_tiles = [held.tile([P, TOKENS], BF16, name=f"base_tile{a}") for a in range(BLOCKS)]
+        for a in range(BLOCKS):
+            queue = nc.sync if a % 2 == 0 else nc.scalar
+            queue.dma_start(base_tiles[a][:], base[a * P : (a + 1) * P, :])
         offsets = held.tile([P, LISTED // 16], U16, name="offsets")
         nc.sync.dma_start(offsets[:], offs)
         x_tile = held.tile([P, LISTED], BF16, name="x_tile")
         nc.sync.dma_start(x_tile[:], x)
-        base_tile = held.tile([P, BLOCKS, TOKENS], BF16, name="base_tile")
-        nc.scalar.dma_start(base_tile[:], base_blocks)
+        w_tile = held.tile([P, FEATURES], BF16, name="w_tile")
+        nc.scalar.dma_start(w_tile[:], w)
         identity = held.tile([P, P], BF16, name="identity")
         make_identity(nc, identity[:])
-        w_tile = held.tile([P, FEATURES], BF16, name="w_tile")
-        nc.gpsimd.dma_start(w_tile[:], w)
 
         windows = [banks.tile([P, TOKENS], F32, name=f"window{a}") for a in range(BLOCKS)]
 
         for a in range(BLOCKS):
-            nc.tensor.matmul(windows[a][:], identity[:], base_tile[:, a, :], start=True, stop=False)
+            nc.tensor.matmul(windows[a][:], identity[:], base_tiles[a][:], start=True, stop=False)
 
         for a in range(BLOCKS):
             nc.tensor.matmul(
@@ -46,5 +47,9 @@ def tile_scatter_matmul_kernel(tc, base, x, w, offs, out):
 
         for a in range(BLOCKS):
             z_tile = held.tile([P, TOKENS], F32, name=f"z_tile{a}")
-            nc.vector.tensor_copy(z_tile[:], windows[a][:])
-            nc.sync.dma_start(out[a * P : (a + 1) * P, :], z_tile[:])
+            if a % 2 == 0:
+                nc.vector.tensor_copy(z_tile[:], windows[a][:])
+                nc.sync.dma_start(out[a * P : (a + 1) * P, :], z_tile[:])
+            else:
+                nc.scalar.copy(z_tile[:], windows[a][:])
+                nc.scalar.dma_start(out[a * P : (a + 1) * P, :], z_tile[:])

@@ -8,6 +8,7 @@ TOKENS = 256
 FEATURES = 512
 LISTED = 128
 BLOCKS = FEATURES // P
+WARM_MATMULS = 8
 
 FLOPS = 2 * P * FEATURES * LISTED
 
@@ -18,6 +19,12 @@ def tile_scatter_matmul_kernel(tc, base, x, w, offs, out):
         tc.tile_pool(name="held", bufs=1) as held,
         tc.psum_pool(name="banks", bufs=1) as banks,
     ):
+        zeros = held.tile([P, P], BF16, name="zeros")
+        nc.vector.memset(zeros[:], 0.0)
+        unread = banks.tile([P, P], F32, name="unread")
+        for i in range(WARM_MATMULS):
+            nc.tensor.matmul(unread[:], zeros[:], zeros[:], start=True, stop=True)
+
         base_tiles = [held.tile([P, TOKENS], BF16, name=f"base_tile{a}") for a in range(BLOCKS)]
         for a in range(BLOCKS):
             queue = nc.sync if a % 2 == 0 else nc.scalar

@@ -34,7 +34,8 @@ def tile_scatter_matmul_kernel(tc, base, x, w, offs, out):
         x_tile = held.tile([P, LISTED], BF16, name="x_tile")
         nc.sync.dma_start(x_tile[:], x)
         w_tile = held.tile([P, FEATURES], BF16, name="w_tile")
-        nc.scalar.dma_start(w_tile[:], w)
+        nc.scalar.dma_start(w_tile[:, 0:P], w[:, 0:P])
+        nc.scalar.dma_start(w_tile[:, P:FEATURES], w[:, P:FEATURES])
         identity = held.tile([P, P], BF16, name="identity")
         make_identity(nc, identity[:])
 

@@ -9,6 +9,7 @@ FEATURES = 512
 LISTED = 128
 BLOCKS = FEATURES // P
 WARM_MATMULS = 8
+ROW_ALIGN = 256
 
 FLOPS = 2 * P * FEATURES * LISTED
 
@@ -25,15 +26,17 @@ def tile_scatter_matmul_kernel(tc, base, x, w, offs, out):
         for i in range(WARM_MATMULS):
             nc.tensor.matmul(unread[:], zeros[:], zeros[:], start=True, stop=True)
 
-        base_tiles = [held.tile([P, TOKENS], BF16, name=f"base_tile{a}") for a in range(BLOCKS)]
+        base_tiles = [
+            held.tile([P, TOKENS], BF16, name=f"base_tile{a}", align_bytes=ROW_ALIGN) for a in range(BLOCKS)
+        ]
         for a in range(BLOCKS):
             queue = nc.sync if a % 2 == 0 else nc.scalar
             queue.dma_start(base_tiles[a][:], base[a * P : (a + 1) * P, :])
         offsets = held.tile([P, LISTED // 16], U16, name="offsets")
         nc.sync.dma_start(offsets[:], offs)
-        x_tile = held.tile([P, LISTED], BF16, name="x_tile")
+        x_tile = held.tile([P, LISTED], BF16, name="x_tile", align_bytes=ROW_ALIGN)
         nc.sync.dma_start(x_tile[:], x)
-        w_tile = held.tile([P, FEATURES], BF16, name="w_tile")
+        w_tile = held.tile([P, FEATURES], BF16, name="w_tile", align_bytes=ROW_ALIGN)
         nc.scalar.dma_start(w_tile[:, 0:P], w[:, 0:P])
         nc.scalar.dma_start(w_tile[:, P:FEATURES], w[:, P:FEATURES])
         identity = held.tile([P, P], BF16, name="identity")
@@ -54,7 +57,7 @@ def tile_scatter_matmul_kernel(tc, base, x, w, offs, out):
             )
 
         for a in range(BLOCKS):
-            z_tile = held.tile([P, TOKENS], F32, name=f"z_tile{a}")
+            z_tile = held.tile([P, TOKENS], F32, name=f"z_tile{a}", align_bytes=ROW_ALIGN)
             if a % 2 == 0:
                 nc.vector.tensor_copy(z_tile[:], windows[a][:])
                 nc.sync.dma_start(out[a * P : (a + 1) * P, :], z_tile[:])

@@ -32,7 +32,7 @@ def tile_scatter_matmul_kernel(tc, base, x, w, offs, out):
         for a in range(BLOCKS):
             queue = nc.sync if a % 2 == 0 else nc.scalar
             queue.dma_start(base_tiles[a][:], base[a * P : (a + 1) * P, :])
-        offsets = held.tile([P, LISTED // 16], U16, name="offsets")
+        offsets = held.tile([P, LISTED // 16], U16, name="offsets", align_bytes=ROW_ALIGN)
         nc.sync.dma_start(offsets[:], offs)
         x_tile = held.tile([P, LISTED], BF16, name="x_tile", align_bytes=ROW_ALIGN)
         nc.sync.dma_start(x_tile[:], x)

@@ -30,7 +30,7 @@ def tile_scatter_matmul_kernel(tc, base, x, w, offs, out):
             held.tile([P, TOKENS], BF16, name=f"base_tile{a}", align_bytes=ROW_ALIGN) for a in range(BLOCKS)
         ]
         for a in range(BLOCKS):
-            queue = nc.sync if a % 2 == 0 else nc.scalar
+            queue = nc.scalar if a == 1 else nc.sync
             queue.dma_start(base_tiles[a][:], base[a * P : (a + 1) * P, :])
         offsets = held.tile([P, LISTED // 16], U16, name="offsets", align_bytes=ROW_ALIGN)
         nc.sync.dma_start(offsets[:], offs)
@@ -38,7 +38,7 @@ def tile_scatter_matmul_kernel(tc, base, x, w, offs, out):
         nc.sync.dma_start(x_tile[:], x)
         w_tile = held.tile([P, FEATURES], BF16, name="w_tile", align_bytes=ROW_ALIGN)
         nc.scalar.dma_start(w_tile[:, 0:P], w[:, 0:P])
-        nc.scalar.dma_start(w_tile[:, P:FEATURES], w[:, P:FEATURES])
+        nc.sync.dma_start(w_tile[:, P:FEATURES], w[:, P:FEATURES])
         identity = held.tile([P, P], BF16, name="identity")
         make_identity(nc, identity[:])
 

@@ -9,7 +9,7 @@ FEATURES = 512
 LISTED = 128
 BLOCKS = FEATURES // P
 WARM_MATMULS = 8
-ROW_ALIGN = 256
+ROW_ALIGN = 1024
 
 FLOPS = 2 * P * FEATURES * LISTED
 

import concourse.mybir as mybir
from concourse.masks import make_identity

BF16, F32, U16 = mybir.dt.bfloat16, mybir.dt.float32, mybir.dt.uint16

P = 128
TOKENS = 256
FEATURES = 512
LISTED = 128
BLOCKS = FEATURES // P
WARM_MATMULS = 8
ROW_ALIGN = 1024

FLOPS = 2 * P * FEATURES * LISTED


def tile_scatter_matmul_kernel(tc, base, x, w, offs, out):
    nc = tc.nc
    with (
        tc.tile_pool(name="held", bufs=1) as held,
        tc.psum_pool(name="banks", bufs=1) as banks,
    ):
        zeros = held.tile([P, P], BF16, name="zeros")
        nc.vector.memset(zeros[:], 0.0)
        unread = banks.tile([P, P], F32, name="unread")
        for i in range(WARM_MATMULS):
            nc.tensor.matmul(unread[:], zeros[:], zeros[:], start=True, stop=True)

        base_tiles = [
            held.tile([P, TOKENS], BF16, name=f"base_tile{a}", align_bytes=ROW_ALIGN) for a in range(BLOCKS)
        ]
        for a in range(BLOCKS):
            queue = nc.scalar if a == 1 else nc.sync
            queue.dma_start(base_tiles[a][:], base[a * P : (a + 1) * P, :])
        offsets = held.tile([P, LISTED // 16], U16, name="offsets", align_bytes=ROW_ALIGN)
        nc.sync.dma_start(offsets[:], offs)
        x_tile = held.tile([P, LISTED], BF16, name="x_tile", align_bytes=ROW_ALIGN)
        nc.sync.dma_start(x_tile[:], x)
        w_tile = held.tile([P, FEATURES], BF16, name="w_tile", align_bytes=ROW_ALIGN)
        nc.scalar.dma_start(w_tile[:, 0:P], w[:, 0:P])
        nc.sync.dma_start(w_tile[:, P:FEATURES], w[:, P:FEATURES])
        identity = held.tile([P, P], BF16, name="identity")
        make_identity(nc, identity[:])

        windows = [banks.tile([P, TOKENS], F32, name=f"window{a}") for a in range(BLOCKS)]

        for a in range(BLOCKS):
            nc.tensor.matmul(windows[a][:], identity[:], base_tiles[a][:], start=True, stop=False)

        for a in range(BLOCKS):
            nc.tensor.matmul(
                windows[a][:].indirect(offsets[:]),
                w_tile[:, a * P : (a + 1) * P],
                x_tile[:],
                start=False,
                stop=True,
            )

        for a in range(BLOCKS):
            z_tile = held.tile([P, TOKENS], F32, name=f"z_tile{a}", align_bytes=ROW_ALIGN)
            if a % 2 == 0:
                nc.vector.tensor_copy(z_tile[:], windows[a][:])
                nc.sync.dma_start(out[a * P : (a + 1) * P, :], z_tile[:])
            else:
                nc.scalar.copy(z_tile[:], windows[a][:])
                nc.scalar.dma_start(out[a * P : (a + 1) * P, :], z_tile[:])
